import numpy as np
import ml_dtypes


def mxq(x, axis, fmt="e4m3"):
    dtype, down = {"e4m3": (ml_dtypes.float8_e4m3fn, 7), "e5m2": (ml_dtypes.float8_e5m2, 14)}[fmt]
    v = np.moveaxis(np.asarray(x, np.float32).astype(ml_dtypes.bfloat16).astype(np.float64), axis, -1)
    blocks = v.reshape(v.shape[:-1] + (-1, 32))
    amax = np.abs(blocks).max(-1, keepdims=True)
    byte = np.maximum(np.where(amax > 0, np.frexp(amax)[1] - 1 + 127, 0) - down, 1)
    scale = np.exp2(byte - 127.0)
    codes = (blocks / scale).astype(np.float32).astype(dtype).astype(np.float64)
    return np.moveaxis((codes * scale).reshape(v.shape), -1, axis)


WIDE = False


def mx_kscale(k):
    if not WIDE:
        return np.ones(k)
    levels = np.array([10, -10, 5, -5, 0])
    if k % 512:
        return np.exp2(np.random.permutation(np.resize(levels, k // 32))).repeat(32)
    a = np.empty((k // 512, 16))
    for p in range(k // 512):
        a[p, :8] = np.random.permutation(np.resize(levels, 8))
        for g in range(8):
            far = levels[np.abs(levels - a[p, g]) >= 10]
            a[p, g + 8] = far[np.random.randint(len(far))]
    return np.exp2(a.ravel()).repeat(32)


def f64(x):
    return np.asarray(x).astype(np.float64)


def striped(idx):
    return np.tile(idx.reshape(-1, 16).T, (8, 1)).astype(np.uint16)


def unstriped(offs):
    return offs[:16].T.reshape(-1).astype(np.int64)


def striped8(idx):
    return np.concatenate([x.reshape(-1, 16).T for x in idx]).astype(np.uint16)


def runs(offs, k):
    lists = np.stack([offs[16 * r : 16 * r + 16].T.reshape(-1) for r in range(8)]).astype(np.int64)
    return lists[np.arange(k) % 512 // 64]


def pack_weight(w):
    k, n = w.shape
    w = f64(np.asarray(w, np.float32).astype(ml_dtypes.bfloat16)).reshape(k // 32, 32, n)
    amax = np.abs(w).max(1)
    byte = np.clip(np.where(amax > 0, np.frexp(amax)[1] - 1 + 127 - 7, 1), 1, 254)
    scaled = (w * np.exp2(127.0 - byte)[:, None, :]).reshape(k, n).astype(np.float32)
    words = np.ascontiguousarray(scaled.reshape(k // 512, 128, 4, n).transpose(0, 1, 3, 2)).astype(ml_dtypes.float8_e4m3fn).view(np.uint8)
    return words, np.ascontiguousarray(byte.astype(np.uint8).reshape(k // 512, 16, n))


def unpack_weight(words, scales):
    g, p, n, _ = words.shape
    vals = np.ascontiguousarray(words).view(ml_dtypes.float8_e4m3fn).astype(np.float64) * np.repeat(np.exp2(scales.astype(np.float64) - 127.0), 8, axis=1)[..., None]
    return vals.transpose(0, 1, 3, 2).reshape(g * 512, n)

def planes(y):
    n, m = y.shape
    v = y.astype(np.float32).astype(ml_dtypes.bfloat16).astype(np.float64).reshape(n // 32, 32, m)
    top = np.abs(v).max(1)
    byte = np.clip(np.where(top > 0, np.frexp(top)[1] - 1 + 127 - 7, 1), 1, 254)
    codes = (v * np.exp2(127.0 - byte)[:, None, :]).reshape(n, m).astype(np.float32).astype(ml_dtypes.float8_e4m3fn).view(np.uint8)
    words = codes.reshape(n // 512, 128, 4, m).transpose(0, 1, 3, 2)
    return np.ascontiguousarray(words), np.ascontiguousarray(byte.astype(np.uint8).reshape(n // 512, 16, m))


K, T, S, N, H, W = 512, 2048, 512, 512, 512, 256


def setup_inputs():
    n = np.random.standard_normal
    s = mx_kscale(K)[:, None]
    u = mx_kscale(H)
    packed_xT = pack_weight(n((K, T)) * s)
    packed_w1 = pack_weight(n((K, H)) / np.sqrt(K) / s)
    packed_w2 = pack_weight(n((H, N)) / np.sqrt(H) / u[:, None])
    packed_w3 = pack_weight(n((H, N)) / np.sqrt(H) / u[:, None])
    perm = np.stack([np.random.permutation(S) for _ in range(8)])
    return {
        "x_words": packed_xT[0],
        "x_scales": packed_xT[1],
        "w1_words": packed_w1[0],
        "w1_scales": packed_w1[1],
        "gn": (np.random.uniform(0.5, 1.5, (H, 1)) * u[:, None]).astype(np.float32),
        "w2_words": packed_w2[0],
        "w2_scales": packed_w2[1],
        "gm": (np.random.uniform(0.5, 1.5, (H, 1)) * u[:, None]).astype(np.float32),
        "w3_words": packed_w3[0],
        "w3_scales": packed_w3[1],
        "offs": striped(np.random.permutation(T)[:S]),
        "n1": striped8(np.stack([np.random.permutation(S) for _ in range(8)])),
        "n2": striped8(np.stack([np.random.permutation(S) for _ in range(8)])),
        "n3": striped8(np.stack([np.random.permutation(S) for _ in range(8)])),
        "n4": striped8(np.stack([np.random.permutation(S) for _ in range(8)])),
        "n5": striped8(perm[:, :W]),
        "n6": striped8(perm[:, W:]),
        "n7": striped8(np.stack([np.random.permutation(S)[:W] for _ in range(8)])),
        "n8": striped8(np.stack([np.random.permutation(S)[:W] for _ in range(8)])),
    }


def reference(x_words, x_scales, w1_words, w1_scales, gn, w2_words, w2_scales, gm, w3_words, w3_scales, offs, n1, n2, n3, n4, n5, n6, n7, n8):
    xq = unpack_weight(x_words, x_scales)[:, unstriped(offs)]
    y = unpack_weight(w1_words, w1_scales).T @ xq
    pa = y[np.arange(H)[:, None], runs(n5, H)]
    pb = y[np.arange(H)[:, None], runs(n6, H)]
    rb = pa * pb
    ra = pa + pb
    ds = np.zeros((H, S))
    ds[np.arange(H)[:, None], runs(n5, H)] = ra
    dt = ds.copy()
    dt[np.arange(H)[:, None], runs(n6, H)] = rb
    z2 = f64(gm) * dt
    b = unpack_weight(w3_words, w3_scales).T @ mxq(z2, 0, "e4m3")
    z = f64(gn) * (0.75 * ((y[np.arange(H)[:, None], runs(n1, H)]) * (y[np.arange(H)[:, None], runs(n2, H)]) - ((y[np.arange(H)[:, None], runs(n3, H)]) * (y[np.arange(H)[:, None], runs(n4, H)]))))
    a = unpack_weight(w2_words, w2_scales).T @ mxq(z, 0, "e4m3")
    ra2 = b[np.arange(N)[:, None], runs(n8, N)] - (0.5 * (a[np.arange(N)[:, None], runs(n7, N)]))
    out = a.copy()
    out[np.arange(N)[:, None], runs(n7, N)] = ra2
    return (out,) + planes(out)

@@ -1,0 +1,202 @@
+from contextlib import ExitStack
+
+import concourse.mybir as mybir
+from concourse.masks import make_identity
+
+F32, BF16 = mybir.dt.float32, mybir.dt.bfloat16
+I32, U32, U16, U8 = mybir.dt.int32, mybir.dt.uint32, mybir.dt.uint16, mybir.dt.uint8
+FP8X4 = mybir.dt.float8_e4m3fn_x4
+MULT, ADD = mybir.AluOpType.mult, mybir.AluOpType.add
+COPY = mybir.ActivationFunctionType.Copy
+
+P, PACK = 128, 4
+T, S, W = 2048, 512, 256
+CHUNKS = ((0, 256), (256, 512))
+FLOPS = 3 * 2 * 512 * 512 * 512
+
+
+def tile_picked_forkputbdetbond_none_po_kernel(
+    tc, x_words, x_scales, w1_words, w1_scales, gn, w2_words, w2_scales, gm, w3_words, w3_scales,
+    offs, n1, n2, n3, n4, n5, n6, n7, n8, out_0, out_1, out_2,
+):
+    nc = tc.nc
+    with ExitStack() as ctx:
+        keep = ctx.enter_context(tc.tile_pool(name="keep", bufs=1))
+        ring = ctx.enter_context(tc.tile_pool(name="ring", bufs=2))
+        mm = ctx.enter_context(tc.psum_pool(name="mm", bufs=4))
+        fwd = ctx.enter_context(tc.psum_pool(name="fwd", bufs=3))
+        back = ctx.enter_context(tc.psum_pool(name="back", bufs=1))
+
+        def load_list(src, name):
+            tile = keep.tile([P, src.shape[1]], U16, name=name)
+            nc.sync.dma_start(tile[:], src)
+            return tile
+
+        def load_words(dst, src):
+            nc.sync.dma_start(dst, src[0].rearrange("p n r -> p (n r)").bitcast(I32))
+
+        def load_scales(dst, src, first, quadrants):
+            for q in quadrants:
+                nc.sync.dma_start(dst[32 * q + first : 32 * q + first + 4, :].bitcast(I32), src[0, 4 * q : 4 * q + 4, :].bitcast(I32))
+
+        xs_all = keep.tile([P, T], U8, align_bytes=64)
+        ws_raw = keep.tile([P, S], U8, align_bytes=64)
+        nc.vector.memset(xs_all[:].bitcast(I32), 0)
+        nc.gpsimd.memset(ws_raw[:].bitcast(I32), 0)
+
+        xw_all = keep.tile([P, T], I32, align_bytes=64)
+        w1w_raw = keep.tile([P, S], I32, name="w1w_raw", tag="wraw", align_bytes=64)
+        gn_sb = keep.tile([P, PACK], F32)
+        gm_sb = keep.tile([P, PACK], F32)
+
+        load_words(w1w_raw[:], w1_words)
+        l_offs = load_list(offs, "l_offs")
+        load_scales(ws_raw, w1_scales, 0, (0,))
+        load_scales(xs_all, x_scales, 0, range(4))
+        load_words(xw_all[:], x_words)
+        load_scales(ws_raw, w1_scales, 0, (1, 2, 3))
+        l5 = load_list(n5, "l5")
+        l6 = load_list(n6, "l6")
+        nc.sync.dma_start(gn_sb[:], gn.rearrange("(p t) o -> p (t o)", t=PACK))
+        nc.sync.dma_start(gm_sb[:], gm.rearrange("(p t) o -> p (t o)", t=PACK))
+        l1 = load_list(n1, "l1")
+        l3 = load_list(n3, "l3")
+        l2 = load_list(n2, "l2")
+        l4 = load_list(n4, "l4")
+        l8 = load_list(n8, "l8")
+        l7 = load_list(n7, "l7")
+
+        ident = keep.tile([P, P], F32)
+        make_identity(nc, ident[:])
+        gain = keep.tile([P, PACK], F32)
+        nc.scalar.activation(gain[:], gn_sb[:], COPY, scale=0.75)
+
+        def deal(raw, dtype, name):
+            dealt = keep.tile([P, S], dtype, name=name, align_bytes=64)
+            nc.vector.tensor_copy(dealt[:].rearrange("p (t m) -> p t m", t=PACK), raw[:].rearrange("p (m t) -> p t m", t=PACK))
+            return dealt
+
+        w1w = deal(w1w_raw, I32, "w1w")
+        w1s = deal(ws_raw, U8, "w1s")
+        w23w_raw = keep.tile([P, 2, S], I32, name="w23w_raw", tag="wraw", align_bytes=64)
+        load_words(w23w_raw[:, 0, :], w2_words)
+        load_words(w23w_raw[:, 1, :], w3_words)
+        load_scales(ws_raw, w2_scales, 4, range(4))
+        load_scales(ws_raw, w3_scales, 8, range(4))
+
+        xs = keep.tile([P, S], U8, align_bytes=64)
+        xw = keep.tile([P, S], U32, align_bytes=64)
+        nc.vector.tensor_copy(xs[:], xs_all[:].indirect(l_offs[:]))
+        for h in range(2):
+            nc.vector.tensor_copy(xw[:, h * W : (h + 1) * W], xw_all[:].bitcast(U32).indirect(l_offs[:, h * 16 : (h + 1) * 16]))
+
+        def product(out, ww, ws, first, t, rw, rs):
+            cols = slice(t * P, (t + 1) * P)
+            nc.tensor.matmul_mx(out=out, lhsT=ww[:, cols].bitcast(FP8X4), lhsT_scale=ws[first:P, cols],
+                                rhs=rw.bitcast(FP8X4), rhs_scale=rs, start=True, stop=True)
+
+        y, yg = [], []
+        y_ps = []
+        for t in range(PACK):
+            ps = mm.tile([P, S], F32, name="ps", tag="ps")
+            y.append(keep.tile([P, S], F32, name=f"y{t}"))
+            for h in range(2):
+                half = slice(h * W, (h + 1) * W)
+                product(ps[:, half], w1w, w1s, 0, t, xw[:, half], xs[:, half])
+            nc.scalar.copy(y[t][:], ps[:])
+            y_ps.append(ps)
+        for t in range(PACK):
+            yg.append(keep.tile([P, S], F32, name=f"yg{t}"))
+            nc.scalar.activation(yg[t][:], y_ps[t][:], COPY, scale=gain[:, t : t + 1])
+
+        w23w = keep.tile([P, 2, S], I32, align_bytes=64)
+        nc.vector.tensor_copy(w23w[:].rearrange("p w (t m) -> p w t m", t=PACK), w23w_raw[:].rearrange("p w (m t) -> p w t m", t=PACK))
+        w2w, w3w = w23w[:, 0, :], w23w[:, 1, :]
+        w23s = deal(ws_raw, U8, "w23s")
+
+        z2 = keep.tile([P, S, PACK], BF16, align_bytes=64)
+        for t in range(PACK):
+            pa = ring.tile([P, W], F32, name="pa")
+            pb = ring.tile([P, W], F32, name="pb")
+            nc.vector.tensor_copy(pa[:], y[t][:].indirect(l5[:]))
+            nc.vector.tensor_copy(pb[:], y[t][:].indirect(l6[:]))
+            dt = keep.tile([P, S], F32, name=f"dt{t}")
+            nc.vector.tensor_tensor(dt[:].indirect(l5[:]), pa[:], pb[:], ADD)
+            nc.vector.tensor_tensor(dt[:].indirect(l6[:]), pa[:], pb[:], MULT)
+            nc.scalar.activation(z2[:, :, t], dt[:], COPY, scale=gm_sb[:, t : t + 1])
+        z2w = keep.tile([P, S], U32, align_bytes=64)
+        z2s = keep.tile([P, S], U8, align_bytes=64)
+        nc.vector.quantize_mx(out=z2w[:].bitcast(FP8X4), scales=z2s[:], in_=z2[:].rearrange("p n t -> p (n t)"))
+        b = []
+        for t in range(PACK):
+            ps = mm.tile([P, S], F32, name="ps", tag="ps")
+            product(ps[:], w3w, w23s, 8, t, z2w[:], z2s[:])
+            b.append(keep.tile([P, S], F32, name=f"b{t}"))
+            nc.scalar.copy(b[t][:], ps[:])
+
+        a = [keep.tile([P, S], F32, name=f"a{t}") for t in range(PACK)]
+        for c0, c1 in CHUNKS:
+            n = c1 - c0
+            ent = slice(c0 // 16, c1 // 16)
+            sums = [fwd.tile([P, PACK, P], F32, name="sums", tag="sums") for j in range(n // P)]
+            for t in range(PACK):
+                g1 = ring.tile([P, n], F32, name="g1")
+                g3 = ring.tile([P, n], F32, name="g3")
+                p12 = ring.tile([P, n], F32, name="p12")
+                p34 = ring.tile([P, n], F32, name="p34")
+                nc.vector.tensor_copy(g1[:], yg[t][:].indirect(l1[:, ent]))
+                nc.vector.tensor_scalar(g3[:], yg[t][:].indirect(l3[:, ent]), -1.0, 0.0, MULT, ADD)
+                nc.vector.tensor_tensor(p12[:], y[t][:].indirect(l2[:, ent]), g1[:], MULT)
+                nc.vector.tensor_tensor(p34[:], y[t][:].indirect(l4[:, ent]), g3[:], MULT)
+                for j in range(n // P):
+                    blk = slice(j * P, (j + 1) * P)
+                    nc.tensor.matmul(sums[j][:, t, :], p12[:, blk], ident[:], start=True, stop=False, is_transpose=True)
+                    nc.tensor.matmul(sums[j][:, t, :], p34[:, blk], ident[:], start=False, stop=True, is_transpose=True)
+            z = ring.tile([P, n, PACK], BF16, name="z", align_bytes=64)
+            turned = back.tile([P, n // P, 2, P], F32, name="turned")
+            for j in range(n // P):
+                zt = ring.tile([P, 2, P, 2], BF16, name="zt")
+                nc.scalar.copy(zt[:], sums[j][:].rearrange("s (u e) p -> s u p e", e=2))
+                words = zt[:].rearrange("s u p e -> s (u p e)").bitcast(F32)
+                for u in range(2):
+                    nc.tensor.transpose(turned[:, j, u, :], words[:, u * P : (u + 1) * P], ident[:])
+            nc.scalar.copy(
+                z[:].rearrange("p n t -> p (n t)").bitcast(F32).rearrange("p (j s u) -> p j s u", u=2, s=P),
+                turned[:].rearrange("p j u s -> p j s u"),
+            )
+            zw = ring.tile([P, n], U32, name="zw", align_bytes=64)
+            zs = ring.tile([P, n], U8, name="zs", align_bytes=64)
+            nc.vector.quantize_mx(out=zw[:].bitcast(FP8X4), scales=zs[:], in_=z[:].rearrange("p n t -> p (n t)"))
+            for t in range(PACK):
+                ps = mm.tile([P, n], F32, name="ps", tag="ps")
+                product(ps[:], w2w, w23s, 4, t, zw[:], zs[:])
+                nc.scalar.copy(a[t][:, c0:c1], ps[:])
+
+        gb = []
+        for t in range(PACK):
+            gb.append(keep.tile([P, W], F32, name=f"gb{t}"))
+            nc.vector.tensor_copy(gb[t][:], b[t][:].indirect(l8[:]))
+        res = [keep.tile([P, W, PACK], BF16, name=f"res{h}", align_bytes=64) for h in range(2)]
+        rows = out_0.rearrange("(p t) n -> p t n", t=PACK)
+        ga = []
+        for t in range(PACK):
+            ga.append(keep.tile([P, W], F32, name=f"ga{t}"))
+            nc.vector.tensor_scalar(ga[t][:], a[t][:].indirect(l7[:]), -0.5, 0.0, MULT, ADD)
+        for t in range(PACK):
+            nc.vector.tensor_tensor(a[t][:].indirect(l7[:]), gb[t][:], ga[t][:], ADD)
+            nc.sync.dma_start(rows[:, t, :], a[t][:])
+            if t < 2:
+                nc.scalar.copy(res[1][:, :, t], a[t][:, W:S])
+            else:
+                nc.vector.tensor_copy(res[1][:, :, t], a[t][:, W:S])
+            nc.scalar.copy(res[0][:, :, t], a[t][:, 0:W])
+        rw = keep.tile([P, S], U32, align_bytes=64)
+        rs = keep.tile([P, S], U8, align_bytes=64)
+        words_out = out_1[0].rearrange("p n r -> p (n r)").bitcast(I32)
+        for h in (1, 0):
+            half = slice(h * W, (h + 1) * W)
+            nc.vector.quantize_mx(out=rw[:, half].bitcast(FP8X4), scales=rs[:, half], in_=res[h][:].rearrange("p n t -> p (n t)"))
+            nc.sync.dma_start(words_out[:, half], rw[:, half].bitcast(I32))
+        for q in range(4):
+            queue = nc.scalar if q % 2 else nc.sync
+            queue.dma_start(out_2[0, 4 * q : 4 * q + 4, :].bitcast(I32), rs[32 * q : 32 * q + 4, :].bitcast(I32))

@@ -11,7 +11,6 @@ COPY = mybir.ActivationFunctionType.Copy
 
 P, PACK = 128, 4
 T, S, W = 2048, 512, 256
-CHUNKS = ((0, 256), (256, 512))
 FLOPS = 3 * 2 * 512 * 512 * 512
 
 
@@ -24,8 +23,7 @@ def tile_picked_forkputbdetbond_none_po_kernel(
         keep = ctx.enter_context(tc.tile_pool(name="keep", bufs=1))
         ring = ctx.enter_context(tc.tile_pool(name="ring", bufs=2))
         mm = ctx.enter_context(tc.psum_pool(name="mm", bufs=4))
-        fwd = ctx.enter_context(tc.psum_pool(name="fwd", bufs=3))
-        back = ctx.enter_context(tc.psum_pool(name="back", bufs=1))
+        fwd = ctx.enter_context(tc.psum_pool(name="fwd", bufs=4))
 
         def load_list(src, name):
             tile = keep.tile([P, src.shape[1]], U16, name=name)
@@ -40,49 +38,51 @@ def tile_picked_forkputbdetbond_none_po_kernel(
                 nc.sync.dma_start(dst[32 * q + first : 32 * q + first + 4, :].bitcast(I32), src[0, 4 * q : 4 * q + 4, :].bitcast(I32))
 
         xs_all = keep.tile([P, T], U8, align_bytes=64)
-        ws_raw = keep.tile([P, S], U8, align_bytes=64)
+        w1s_raw = keep.tile([P, S], U8, align_bytes=64)
+        w23s_raw = keep.tile([P, S], U8, align_bytes=64)
         nc.vector.memset(xs_all[:].bitcast(I32), 0)
-        nc.gpsimd.memset(ws_raw[:].bitcast(I32), 0)
+        nc.gpsimd.memset(w1s_raw[:].bitcast(I32), 0)
+        nc.gpsimd.memset(w23s_raw[:].bitcast(I32), 0)
 
         xw_all = keep.tile([P, T], I32, align_bytes=64)
-        w1w_raw = keep.tile([P, S], I32, name="w1w_raw", tag="wraw", align_bytes=64)
+        w1w_raw = keep.tile([P, S], I32, align_bytes=64)
+        w23w_raw = keep.tile([P, 2, S], I32, align_bytes=64)
         gn_sb = keep.tile([P, PACK], F32)
         gm_sb = keep.tile([P, PACK], F32)
 
         load_words(w1w_raw[:], w1_words)
         l_offs = load_list(offs, "l_offs")
-        load_scales(ws_raw, w1_scales, 0, (0,))
+        load_scales(w1s_raw, w1_scales, 0, (0,))
         load_scales(xs_all, x_scales, 0, range(4))
         load_words(xw_all[:], x_words)
-        load_scales(ws_raw, w1_scales, 0, (1, 2, 3))
-        l5 = load_list(n5, "l5")
-        l6 = load_list(n6, "l6")
-        nc.sync.dma_start(gn_sb[:], gn.rearrange("(p t) o -> p (t o)", t=PACK))
-        nc.sync.dma_start(gm_sb[:], gm.rearrange("(p t) o -> p (t o)", t=PACK))
-        l1 = load_list(n1, "l1")
-        l3 = load_list(n3, "l3")
+        load_scales(w1s_raw, w1_scales, 0, (1, 2, 3))
+        nc.gpsimd.dma_start(gn_sb[:], gn.rearrange("(p t) o -> p (t o)", t=PACK))
+        nc.gpsimd.dma_start(gm_sb[:], gm.rearrange("(p t) o -> p (t o)", t=PACK))
         l2 = load_list(n2, "l2")
         l4 = load_list(n4, "l4")
-        l8 = load_list(n8, "l8")
+        load_words(w23w_raw[:, 0, :], w2_words)
+        load_words(w23w_raw[:, 1, :], w3_words)
+        l1 = load_list(n1, "l1")
+        l3 = load_list(n3, "l3")
+        load_scales(w23s_raw, w2_scales, 4, range(4))
+        load_scales(w23s_raw, w3_scales, 8, range(4))
+        l5 = load_list(n5, "l5")
+        l6 = load_list(n6, "l6")
         l7 = load_list(n7, "l7")
+        l8 = load_list(n8, "l8")
 
         ident = keep.tile([P, P], F32)
         make_identity(nc, ident[:])
         gain = keep.tile([P, PACK], F32)
         nc.scalar.activation(gain[:], gn_sb[:], COPY, scale=0.75)
 
-        def deal(raw, dtype, name):
+        def deal(raw, dtype, name, run):
             dealt = keep.tile([P, S], dtype, name=name, align_bytes=64)
-            nc.vector.tensor_copy(dealt[:].rearrange("p (t m) -> p t m", t=PACK), raw[:].rearrange("p (m t) -> p t m", t=PACK))
+            nc.vector.tensor_copy(dealt[:].rearrange("p (t c i) -> p c t i", t=PACK, i=run), raw[:].rearrange("p (c i t) -> p c t i", t=PACK, i=run))
             return dealt
 
-        w1w = deal(w1w_raw, I32, "w1w")
-        w1s = deal(ws_raw, U8, "w1s")
-        w23w_raw = keep.tile([P, 2, S], I32, name="w23w_raw", tag="wraw", align_bytes=64)
-        load_words(w23w_raw[:, 0, :], w2_words)
-        load_words(w23w_raw[:, 1, :], w3_words)
-        load_scales(ws_raw, w2_scales, 4, range(4))
-        load_scales(ws_raw, w3_scales, 8, range(4))
+        w1w = deal(w1w_raw, I32, "w1w", 4)
+        w1s = deal(w1s_raw, U8, "w1s", 16)
 
         xs = keep.tile([P, S], U8, align_bytes=64)
         xw = keep.tile([P, S], U32, align_bytes=64)
@@ -96,94 +96,104 @@ def tile_picked_forkputbdetbond_none_po_kernel(
                                 rhs=rw.bitcast(FP8X4), rhs_scale=rs, start=True, stop=True)
 
         y, yg = [], []
-        y_ps = []
         for t in range(PACK):
-            ps = mm.tile([P, S], F32, name="ps", tag="ps")
-            y.append(keep.tile([P, S], F32, name=f"y{t}"))
-            for h in range(2):
-                half = slice(h * W, (h + 1) * W)
-                product(ps[:, half], w1w, w1s, 0, t, xw[:, half], xs[:, half])
-            nc.scalar.copy(y[t][:], ps[:])
-            y_ps.append(ps)
-        for t in range(PACK):
-            yg.append(keep.tile([P, S], F32, name=f"yg{t}"))
-            nc.scalar.activation(yg[t][:], y_ps[t][:], COPY, scale=gain[:, t : t + 1])
+            y.append(keep.tile([P, 2 * S], F32, name=f"y{t}"))
+            yg.append(keep.tile([P, 2 * S], F32, name=f"yg{t}", tag=f"yg{t}", align_bytes=64))
+            parts = [slice(0, W), slice(W, S)] if t == 0 else [slice(0, S)]
+            banks = []
+            for part in parts:
+                ps = mm.tile([P, part.stop - part.start], F32, name="ps", tag="ps")
+                product(ps[:], w1w, w1s, 0, t, xw[:, part], xs[:, part])
+                nc.scalar.copy(y[t][:, part], ps[:])
+                banks.append(ps)
+            for part, ps in zip(parts, banks):
+                nc.scalar.activation(yg[t][:, part], ps[:], COPY, scale=gain[:, t : t + 1])
 
         w23w = keep.tile([P, 2, S], I32, align_bytes=64)
-        nc.vector.tensor_copy(w23w[:].rearrange("p w (t m) -> p w t m", t=PACK), w23w_raw[:].rearrange("p w (m t) -> p w t m", t=PACK))
+        nc.vector.tensor_copy(w23w[:].rearrange("p w (t c i) -> p w c t i", t=PACK, i=4), w23w_raw[:].rearrange("p w (c i t) -> p w c t i", t=PACK, i=4))
         w2w, w3w = w23w[:, 0, :], w23w[:, 1, :]
-        w23s = deal(ws_raw, U8, "w23s")
+        w23s = deal(w23s_raw, U8, "w23s", 16)
 
-        z2 = keep.tile([P, S, PACK], BF16, align_bytes=64)
+        blocks = S // P
+        sums = [fwd.tile([P, PACK, P], F32, name="sums", tag="sums") for j in range(blocks)]
         for t in range(PACK):
-            pa = ring.tile([P, W], F32, name="pa")
-            pb = ring.tile([P, W], F32, name="pb")
-            nc.vector.tensor_copy(pa[:], y[t][:].indirect(l5[:]))
-            nc.vector.tensor_copy(pb[:], y[t][:].indirect(l6[:]))
-            dt = keep.tile([P, S], F32, name=f"dt{t}")
-            nc.vector.tensor_tensor(dt[:].indirect(l5[:]), pa[:], pb[:], ADD)
-            nc.vector.tensor_tensor(dt[:].indirect(l6[:]), pa[:], pb[:], MULT)
-            nc.scalar.activation(z2[:, :, t], dt[:], COPY, scale=gm_sb[:, t : t + 1])
-        z2w = keep.tile([P, S], U32, align_bytes=64)
-        z2s = keep.tile([P, S], U8, align_bytes=64)
-        nc.vector.quantize_mx(out=z2w[:].bitcast(FP8X4), scales=z2s[:], in_=z2[:].rearrange("p n t -> p (n t)"))
-        b = []
-        for t in range(PACK):
-            ps = mm.tile([P, S], F32, name="ps", tag="ps")
-            product(ps[:], w3w, w23s, 8, t, z2w[:], z2s[:])
-            b.append(keep.tile([P, S], F32, name=f"b{t}"))
-            nc.scalar.copy(b[t][:], ps[:])
-
-        a = [keep.tile([P, S], F32, name=f"a{t}") for t in range(PACK)]
-        for c0, c1 in CHUNKS:
-            n = c1 - c0
-            ent = slice(c0 // 16, c1 // 16)
-            sums = [fwd.tile([P, PACK, P], F32, name="sums", tag="sums") for j in range(n // P)]
-            for t in range(PACK):
-                g1 = ring.tile([P, n], F32, name="g1")
-                g3 = ring.tile([P, n], F32, name="g3")
-                p12 = ring.tile([P, n], F32, name="p12")
-                p34 = ring.tile([P, n], F32, name="p34")
-                nc.vector.tensor_copy(g1[:], yg[t][:].indirect(l1[:, ent]))
-                nc.vector.tensor_scalar(g3[:], yg[t][:].indirect(l3[:, ent]), -1.0, 0.0, MULT, ADD)
-                nc.vector.tensor_tensor(p12[:], y[t][:].indirect(l2[:, ent]), g1[:], MULT)
-                nc.vector.tensor_tensor(p34[:], y[t][:].indirect(l4[:, ent]), g3[:], MULT)
-                for j in range(n // P):
-                    blk = slice(j * P, (j + 1) * P)
-                    nc.tensor.matmul(sums[j][:, t, :], p12[:, blk], ident[:], start=True, stop=False, is_transpose=True)
-                    nc.tensor.matmul(sums[j][:, t, :], p34[:, blk], ident[:], start=False, stop=True, is_transpose=True)
-            z = ring.tile([P, n, PACK], BF16, name="z", align_bytes=64)
-            turned = back.tile([P, n // P, 2, P], F32, name="turned")
-            for j in range(n // P):
-                zt = ring.tile([P, 2, P, 2], BF16, name="zt")
-                nc.scalar.copy(zt[:], sums[j][:].rearrange("s (u e) p -> s u p e", e=2))
+            g2 = ring.tile([P, S], F32, name="g2")
+            g4 = ring.tile([P, S], F32, name="g4")
+            p12 = keep.tile([P, S], F32, name=f"p12_{t}")
+            p34 = keep.tile([P, S], F32, name=f"p34_{t}")
+            nc.vector.tensor_copy(g2[:], y[t][:].indirect(l2[:]))
+            nc.vector.tensor_scalar(g4[:], y[t][:].indirect(l4[:]), -1.0, 0.0, MULT, ADD)
+            nc.vector.tensor_tensor(p12[:], yg[t][:].indirect(l1[:]), g2[:], MULT)
+            nc.vector.tensor_tensor(p34[:], yg[t][:].indirect(l3[:]), g4[:], MULT)
+            for j in range(blocks):
+                blk = slice(j * P, (j + 1) * P)
+                nc.tensor.matmul(sums[j][:, t, :], p12[:, blk], ident[:], start=True, stop=False, is_transpose=True)
+                nc.tensor.matmul(sums[j][:, t, :], p34[:, blk], ident[:], start=False, stop=True, is_transpose=True)
+        z = keep.tile([P, S, PACK], BF16, name="z", tag="z", align_bytes=64)
+        z_words = z[:].rearrange("p n t -> p (n t)").bitcast(F32).rearrange("p (h j s u) -> p h j s u", h=2, u=2, s=P)
+        for h in range(2):
+            turned = mm.tile([P, 2, 2, P], F32, name="turned", tag="ps")
+            for j in range(2):
+                zt = keep.tile([P, 2, P, 2], BF16, name=f"zt{h}{j}", tag=f"z2{j}" if h else f"zt{j}", align_bytes=64)
+                nc.scalar.copy(zt[:], sums[2 * h + j][:].rearrange("s (u e) p -> s u p e", e=2))
                 words = zt[:].rearrange("s u p e -> s (u p e)").bitcast(F32)
                 for u in range(2):
                     nc.tensor.transpose(turned[:, j, u, :], words[:, u * P : (u + 1) * P], ident[:])
-            nc.scalar.copy(
-                z[:].rearrange("p n t -> p (n t)").bitcast(F32).rearrange("p (j s u) -> p j s u", u=2, s=P),
-                turned[:].rearrange("p j u s -> p j s u"),
-            )
-            zw = ring.tile([P, n], U32, name="zw", align_bytes=64)
-            zs = ring.tile([P, n], U8, name="zs", align_bytes=64)
-            nc.vector.quantize_mx(out=zw[:].bitcast(FP8X4), scales=zs[:], in_=z[:].rearrange("p n t -> p (n t)"))
-            for t in range(PACK):
-                ps = mm.tile([P, n], F32, name="ps", tag="ps")
-                product(ps[:], w2w, w23s, 4, t, zw[:], zs[:])
-                nc.scalar.copy(a[t][:, c0:c1], ps[:])
-
-        gb = []
+            nc.scalar.copy(z_words[:, h], turned[:].rearrange("p j u s -> p j s u"))
+        zw = keep.tile([P, S], U32, name="zw", tag="zw", align_bytes=64)
+        zs = keep.tile([P, S], U8, align_bytes=64)
+        nc.vector.quantize_mx(out=zw[:].bitcast(FP8X4), scales=zs[:], in_=z[:].rearrange("p n t -> p (n t)"))
+        a = [keep.tile([P, S], F32, name=f"a{t}") for t in range(PACK)]
         for t in range(PACK):
-            gb.append(keep.tile([P, W], F32, name=f"gb{t}"))
-            nc.vector.tensor_copy(gb[t][:], b[t][:].indirect(l8[:]))
+            ps = mm.tile([P, S], F32, name="ps", tag="ps")
+            product(ps[:], w2w, w23s, 4, t, zw[:], zs[:])
+            nc.scalar.copy(a[t][:], ps[:])
+
+        z2 = [keep.tile([P, W, PACK], BF16, name=f"z2{h}", tag=f"z2{h}", align_bytes=64) for h in range(2)]
+        early = keep.tile([P, 4, W], F32, name="early", tag="yg3", align_bytes=64)
+        late = keep.tile([P, 2, W], F32, name="late", tag="yg2", align_bytes=64)
+        pa2 = keep.tile([P, W], F32, name="pa2", tag="z", align_bytes=64)
+        pa3 = keep.tile([P, W], F32, name="pa3", tag="zw", align_bytes=64)
+        pa = [early[:, 0, :], early[:, 2, :], pa2[:], pa3[:]]
+        pb = [early[:, 1, :], early[:, 3, :], late[:, 0, :], late[:, 1, :]]
+        for t in range(PACK):
+            nc.vector.tensor_copy(pa[t], y[t][:].indirect(l5[:]))
+            nc.vector.tensor_copy(pb[t], y[t][:].indirect(l6[:]))
+            dt = keep.tile([P, S], F32, name=f"dt{t}")
+            nc.vector.tensor_tensor(dt[:].indirect(l5[:]), pa[t], pb[t], ADD)
+            nc.vector.tensor_tensor(dt[:].indirect(l6[:]), pa[t], pb[t], MULT)
+            for h in range(2):
+                nc.scalar.activation(z2[h][:, :, t], dt[:, h * W : (h + 1) * W], COPY, scale=gm_sb[:, t : t + 1])
+
+        z2w = keep.tile([P, S], U32, align_bytes=64)
+        z2s = keep.tile([P, S], U8, align_bytes=64)
+        b = [keep.tile([P, S], F32, name=f"b{t}") for t in range(PACK)]
+        ga = []
+
+        def fetch_own(t, tag):
+            ga.append(keep.tile([P, W], F32, name=f"ga{t}", tag=tag, align_bytes=64))
+            nc.vector.tensor_scalar(ga[t][:], a[t][:].indirect(l7[:]), -0.5, 0.0, MULT, ADD)
+
+        fetch_own(0, "zw")
+        fetch_own(1, "yg2")
+        for h in range(2):
+            half = slice(h * W, (h + 1) * W)
+            nc.vector.quantize_mx(out=z2w[:, half].bitcast(FP8X4), scales=z2s[:, half], in_=z2[h][:].rearrange("p n t -> p (n t)"))
+            ps = mm.tile([P, W], F32, name="ps", tag="ps")
+            product(ps[:], w3w, w23s, 8, 0, z2w[:, half], z2s[:, half])
+            nc.scalar.copy(b[0][:, half], ps[:])
+            fetch_own(2 + h, f"z2{h}")
+        for t in range(1, PACK):
+            ps = mm.tile([P, S], F32, name="ps", tag="ps")
+            product(ps[:], w3w, w23s, 8, t, z2w[:], z2s[:])
+            nc.scalar.copy(b[t][:], ps[:])
+
         res = [keep.tile([P, W, PACK], BF16, name=f"res{h}", align_bytes=64) for h in range(2)]
         rows = out_0.rearrange("(p t) n -> p t n", t=PACK)
-        ga = []
         for t in range(PACK):
-            ga.append(keep.tile([P, W], F32, name=f"ga{t}"))
-            nc.vector.tensor_scalar(ga[t][:], a[t][:].indirect(l7[:]), -0.5, 0.0, MULT, ADD)
-        for t in range(PACK):
-            nc.vector.tensor_tensor(a[t][:].indirect(l7[:]), gb[t][:], ga[t][:], ADD)
+            gb = keep.tile([P, W], F32, name=f"gb{t}")
+            nc.vector.tensor_copy(gb[:], b[t][:].indirect(l8[:]))
+            nc.vector.tensor_tensor(a[t][:].indirect(l7[:]), gb[:], ga[t][:], ADD)
             nc.sync.dma_start(rows[:, t, :], a[t][:])
             if t < 2:
                 nc.scalar.copy(res[1][:, :, t], a[t][:, W:S])

@@ -98,7 +98,7 @@ def tile_picked_forkputbdetbond_none_po_kernel(
         y, yg = [], []
         for t in range(PACK):
             y.append(keep.tile([P, 2 * S], F32, name=f"y{t}"))
-            yg.append(keep.tile([P, 2 * S], F32, name=f"yg{t}", tag=f"yg{t}", align_bytes=64))
+            yg.append(keep.tile([P, 2 * S], F32, name=f"yg{t}"))
             parts = [slice(0, W), slice(W, S)] if t == 0 else [slice(0, S)]
             banks = []
             for part in parts:
@@ -117,7 +117,7 @@ def tile_picked_forkputbdetbond_none_po_kernel(
         blocks = S // P
         sums = [fwd.tile([P, PACK, P], F32, name="sums", tag="sums") for j in range(blocks)]
         for t in range(PACK):
-            g2 = ring.tile([P, S], F32, name="g2")
+            g2 = keep.tile([P, S], F32, name=f"g2_{t}", tag=f"g2_{t}", align_bytes=64)
             g4 = ring.tile([P, S], F32, name="g4")
             p12 = keep.tile([P, S], F32, name=f"p12_{t}")
             p34 = keep.tile([P, S], F32, name=f"p34_{t}")
@@ -150,60 +150,88 @@ def tile_picked_forkputbdetbond_none_po_kernel(
             nc.scalar.copy(a[t][:], ps[:])
 
         z2 = [keep.tile([P, W, PACK], BF16, name=f"z2{h}", tag=f"z2{h}", align_bytes=64) for h in range(2)]
-        early = keep.tile([P, 4, W], F32, name="early", tag="yg3", align_bytes=64)
-        late = keep.tile([P, 2, W], F32, name="late", tag="yg2", align_bytes=64)
-        pa2 = keep.tile([P, W], F32, name="pa2", tag="z", align_bytes=64)
-        pa3 = keep.tile([P, W], F32, name="pa3", tag="zw", align_bytes=64)
-        pa = [early[:, 0, :], early[:, 2, :], pa2[:], pa3[:]]
+        early = keep.tile([P, 5, W], F32, name="early", tag="g2_3", align_bytes=64)
+        late = keep.tile([P, 2, W], F32, name="late", tag="z", align_bytes=64)
+        pa2 = keep.tile([P, W], F32, name="pa2", tag="pa2", align_bytes=64)
+        pa = [early[:, 0, :], early[:, 2, :], pa2[:], early[:, 4, :]]
         pb = [early[:, 1, :], early[:, 3, :], late[:, 0, :], late[:, 1, :]]
-        for t in range(PACK):
+        dt = [keep.tile([P, S], F32, name=f"dt{t}", tag=f"dt{t}", align_bytes=64) for t in range(PACK)]
+
+        def fetch_a(t):
             nc.vector.tensor_copy(pa[t], y[t][:].indirect(l5[:]))
+
+        def fetch_b(t):
             nc.vector.tensor_copy(pb[t], y[t][:].indirect(l6[:]))
-            dt = keep.tile([P, S], F32, name=f"dt{t}")
-            nc.vector.tensor_tensor(dt[:].indirect(l5[:]), pa[t], pb[t], ADD)
-            nc.vector.tensor_tensor(dt[:].indirect(l6[:]), pa[t], pb[t], MULT)
+
+        def put_sum(t):
+            nc.vector.tensor_tensor(dt[t][:].indirect(l5[:]), pa[t], pb[t], ADD)
+
+        def put_product(t):
+            nc.vector.tensor_tensor(dt[t][:].indirect(l6[:]), pa[t], pb[t], MULT)
             for h in range(2):
-                nc.scalar.activation(z2[h][:, :, t], dt[:, h * W : (h + 1) * W], COPY, scale=gm_sb[:, t : t + 1])
+                nc.scalar.activation(z2[h][:, :, t], dt[t][:, h * W : (h + 1) * W], COPY, scale=gm_sb[:, t : t + 1])
+
+        fetch_a(0)
+        fetch_b(0)
+        fetch_a(1)
+        put_sum(0)
+        fetch_b(1)
+        put_product(0)
+        fetch_a(2)
+        put_sum(1)
+        fetch_a(3)
+        put_product(1)
+        fetch_b(2)
+        fetch_b(3)
+        put_sum(2)
+        put_sum(3)
+        put_product(2)
+        put_product(3)
 
         z2w = keep.tile([P, S], U32, align_bytes=64)
         z2s = keep.tile([P, S], U8, align_bytes=64)
         b = [keep.tile([P, S], F32, name=f"b{t}") for t in range(PACK)]
-        ga = []
+        own01 = keep.tile([P, 2, W], F32, name="own01", tag="pa2", align_bytes=64)
+        own23 = keep.tile([P, 2, W], F32, name="own23", tag="dt3", align_bytes=64)
+        ga = [own01[:, 0, :], own01[:, 1, :], own23[:, 0, :], own23[:, 1, :]]
 
-        def fetch_own(t, tag):
-            ga.append(keep.tile([P, W], F32, name=f"ga{t}", tag=tag, align_bytes=64))
-            nc.vector.tensor_scalar(ga[t][:], a[t][:].indirect(l7[:]), -0.5, 0.0, MULT, ADD)
+        def fetch_own(t):
+            nc.vector.tensor_scalar(ga[t], a[t][:].indirect(l7[:]), -0.5, 0.0, MULT, ADD)
 
-        fetch_own(0, "zw")
-        fetch_own(1, "yg2")
+        fetch_own(0)
+        fetch_own(1)
         for h in range(2):
             half = slice(h * W, (h + 1) * W)
             nc.vector.quantize_mx(out=z2w[:, half].bitcast(FP8X4), scales=z2s[:, half], in_=z2[h][:].rearrange("p n t -> p (n t)"))
-            ps = mm.tile([P, W], F32, name="ps", tag="ps")
-            product(ps[:], w3w, w23s, 8, 0, z2w[:, half], z2s[:, half])
-            nc.scalar.copy(b[0][:, half], ps[:])
-            fetch_own(2 + h, f"z2{h}")
-        for t in range(1, PACK):
-            ps = mm.tile([P, S], F32, name="ps", tag="ps")
+            for t in range(2):
+                ps = mm.tile([P, W], F32, name="ps", tag="ps")
+                product(ps[:], w3w, w23s, 8, t, z2w[:, half], z2s[:, half])
+                nc.scalar.copy(b[t][:, half], ps[:])
+        fetch_own(2)
+        fetch_own(3)
+        for t in range(2, PACK):
+            ps = fwd.tile([P, S], F32, name="whole", tag="sums")
             product(ps[:], w3w, w23s, 8, t, z2w[:], z2s[:])
             nc.scalar.copy(b[t][:], ps[:])
 
         res = [keep.tile([P, W, PACK], BF16, name=f"res{h}", align_bytes=64) for h in range(2)]
         rows = out_0.rearrange("(p t) n -> p t n", t=PACK)
+        gb = [keep.tile([P, W], F32, name=f"gb{t}") for t in range(PACK)]
+        nc.vector.tensor_copy(gb[0][:], b[0][:].indirect(l8[:]))
         for t in range(PACK):
-            gb = keep.tile([P, W], F32, name=f"gb{t}")
-            nc.vector.tensor_copy(gb[:], b[t][:].indirect(l8[:]))
-            nc.vector.tensor_tensor(a[t][:].indirect(l7[:]), gb[:], ga[t][:], ADD)
+            if t + 1 < PACK:
+                nc.vector.tensor_copy(gb[t + 1][:], b[t + 1][:].indirect(l8[:]))
+            nc.vector.tensor_tensor(a[t][:].indirect(l7[:]), gb[t][:], ga[t], ADD)
             nc.sync.dma_start(rows[:, t, :], a[t][:])
             if t < 2:
                 nc.scalar.copy(res[1][:, :, t], a[t][:, W:S])
-            else:
-                nc.vector.tensor_copy(res[1][:, :, t], a[t][:, W:S])
             nc.scalar.copy(res[0][:, :, t], a[t][:, 0:W])
+        for t in range(2, PACK):
+            nc.vector.tensor_copy(res[1][:, :, t], a[t][:, W:S])
         rw = keep.tile([P, S], U32, align_bytes=64)
         rs = keep.tile([P, S], U8, align_bytes=64)
         words_out = out_1[0].rearrange("p n r -> p (n r)").bitcast(I32)
-        for h in (1, 0):
+        for h in range(2):
             half = slice(h * W, (h + 1) * W)
             nc.vector.quantize_mx(out=rw[:, half].bitcast(FP8X4), scales=rs[:, half], in_=res[h][:].rearrange("p n t -> p (n t)"))
             nc.sync.dma_start(words_out[:, half], rw[:, half].bitcast(I32))

@@ -58,12 +58,12 @@ def tile_picked_forkputbdetbond_none_po_kernel(
         load_scales(w1s_raw, w1_scales, 0, (1, 2, 3))
         nc.gpsimd.dma_start(gn_sb[:], gn.rearrange("(p t) o -> p (t o)", t=PACK))
         nc.gpsimd.dma_start(gm_sb[:], gm.rearrange("(p t) o -> p (t o)", t=PACK))
-        l2 = load_list(n2, "l2")
-        l4 = load_list(n4, "l4")
-        load_words(w23w_raw[:, 0, :], w2_words)
-        load_words(w23w_raw[:, 1, :], w3_words)
         l1 = load_list(n1, "l1")
         l3 = load_list(n3, "l3")
+        load_words(w23w_raw[:, 0, :], w2_words)
+        load_words(w23w_raw[:, 1, :], w3_words)
+        l2 = load_list(n2, "l2")
+        l4 = load_list(n4, "l4")
         load_scales(w23s_raw, w2_scales, 4, range(4))
         load_scales(w23s_raw, w3_scales, 8, range(4))
         l5 = load_list(n5, "l5")
@@ -98,16 +98,16 @@ def tile_picked_forkputbdetbond_none_po_kernel(
         y, yg = [], []
         for t in range(PACK):
             y.append(keep.tile([P, 2 * S], F32, name=f"y{t}"))
-            yg.append(keep.tile([P, 2 * S], F32, name=f"yg{t}"))
+            yg.append(keep.tile([P, 2 * S], F32, name=f"yg{t}", tag=f"yg{t}", align_bytes=64))
             parts = [slice(0, W), slice(W, S)] if t == 0 else [slice(0, S)]
             banks = []
             for part in parts:
                 ps = mm.tile([P, part.stop - part.start], F32, name="ps", tag="ps")
                 product(ps[:], w1w, w1s, 0, t, xw[:, part], xs[:, part])
-                nc.scalar.copy(y[t][:, part], ps[:])
+                nc.scalar.activation(yg[t][:, part], ps[:], COPY, scale=gain[:, t : t + 1])
                 banks.append(ps)
             for part, ps in zip(parts, banks):
-                nc.scalar.activation(yg[t][:, part], ps[:], COPY, scale=gain[:, t : t + 1])
+                nc.scalar.copy(y[t][:, part], ps[:])
 
         w23w = keep.tile([P, 2, S], I32, align_bytes=64)
         nc.vector.tensor_copy(w23w[:].rearrange("p w (t c i) -> p w c t i", t=PACK, i=4), w23w_raw[:].rearrange("p w (c i t) -> p w c t i", t=PACK, i=4))
@@ -117,14 +117,13 @@ def tile_picked_forkputbdetbond_none_po_kernel(
         blocks = S // P
         sums = [fwd.tile([P, PACK, P], F32, name="sums", tag="sums") for j in range(blocks)]
         for t in range(PACK):
-            g2 = keep.tile([P, S], F32, name=f"g2_{t}", tag=f"g2_{t}", align_bytes=64)
-            g4 = ring.tile([P, S], F32, name="g4")
-            p12 = keep.tile([P, S], F32, name=f"p12_{t}")
-            p34 = keep.tile([P, S], F32, name=f"p34_{t}")
+            g1, g2, g3, g4, p12, p34 = [keep.tile([P, S], F32, name=f"{n}_{t}") for n in ("g1", "g2", "g3", "g4", "p12", "p34")]
+            nc.vector.tensor_copy(g1[:], yg[t][:].indirect(l1[:]))
+            nc.vector.tensor_scalar(g3[:], yg[t][:].indirect(l3[:]), -1.0, 0.0, MULT, ADD)
             nc.vector.tensor_copy(g2[:], y[t][:].indirect(l2[:]))
-            nc.vector.tensor_scalar(g4[:], y[t][:].indirect(l4[:]), -1.0, 0.0, MULT, ADD)
-            nc.vector.tensor_tensor(p12[:], yg[t][:].indirect(l1[:]), g2[:], MULT)
-            nc.vector.tensor_tensor(p34[:], yg[t][:].indirect(l3[:]), g4[:], MULT)
+            nc.vector.tensor_copy(g4[:], y[t][:].indirect(l4[:]))
+            nc.gpsimd.tensor_tensor(p12[:], g1[:], g2[:], MULT)
+            nc.gpsimd.tensor_tensor(p34[:], g3[:], g4[:], MULT)
             for j in range(blocks):
                 blk = slice(j * P, (j + 1) * P)
                 nc.tensor.matmul(sums[j][:, t, :], p12[:, blk], ident[:], start=True, stop=False, is_transpose=True)
@@ -150,7 +149,7 @@ def tile_picked_forkputbdetbond_none_po_kernel(
             nc.scalar.copy(a[t][:], ps[:])
 
         z2 = [keep.tile([P, W, PACK], BF16, name=f"z2{h}", tag=f"z2{h}", align_bytes=64) for h in range(2)]
-        early = keep.tile([P, 5, W], F32, name="early", tag="g2_3", align_bytes=64)
+        early = keep.tile([P, 5, W], F32, name="early", tag="yg3", align_bytes=64)
         late = keep.tile([P, 2, W], F32, name="late", tag="z", align_bytes=64)
         pa2 = keep.tile([P, W], F32, name="pa2", tag="pa2", align_bytes=64)
         pa = [early[:, 0, :], early[:, 2, :], pa2[:], early[:, 4, :]]

@@ -9,8 +9,17 @@ FP8X4 = mybir.dt.float8_e4m3fn_x4
 MULT, ADD = mybir.AluOpType.mult, mybir.AluOpType.add
 COPY = mybir.ActivationFunctionType.Copy
 
-P, PACK = 128, 4
-T, S, W = 2048, 512, 256
+P = 128
+PLANES = 4
+QUADRANTS = 4
+T = 2048
+S = 512
+W = 256
+HALVES = (slice(0, W), slice(W, S))
+W1_FIRST, W2_FIRST, W3_FIRST = 0, 4, 8
+LINE_BYTES = 16
+BANKS = 4
+ALIGN = 64
 FLOPS = 3 * 2 * 512 * 512 * 512
 
 
@@ -21,9 +30,8 @@ def tile_picked_forkputbdetbond_none_po_kernel(
     nc = tc.nc
     with ExitStack() as ctx:
         keep = ctx.enter_context(tc.tile_pool(name="keep", bufs=1))
-        ring = ctx.enter_context(tc.tile_pool(name="ring", bufs=2))
-        mm = ctx.enter_context(tc.psum_pool(name="mm", bufs=4))
-        fwd = ctx.enter_context(tc.psum_pool(name="fwd", bufs=4))
+        mm = ctx.enter_context(tc.psum_pool(name="mm", bufs=BANKS))
+        fwd = ctx.enter_context(tc.psum_pool(name="fwd", bufs=BANKS))
 
         def load_list(src, name):
             tile = keep.tile([P, src.shape[1]], U16, name=name)
@@ -33,39 +41,58 @@ def tile_picked_forkputbdetbond_none_po_kernel(
         def load_words(dst, src):
             nc.sync.dma_start(dst, src[0].rearrange("p n r -> p (n r)").bitcast(I32))
 
-        def load_scales(dst, src, first, quadrants):
-            for q in quadrants:
-                nc.sync.dma_start(dst[32 * q + first : 32 * q + first + 4, :].bitcast(I32), src[0, 4 * q : 4 * q + 4, :].bitcast(I32))
+        def load_scales(dst, src, first):
+            for q in range(QUADRANTS):
+                nc.sync.dma_start(
+                    dst[32 * q + first : 32 * q + first + 4, :].bitcast(I32), src[0, 4 * q : 4 * q + 4, :].bitcast(I32)
+                )
 
-        xs_all = keep.tile([P, T], U8, align_bytes=64)
-        w1s_raw = keep.tile([P, S], U8, align_bytes=64)
-        w23s_raw = keep.tile([P, S], U8, align_bytes=64)
-        nc.vector.memset(xs_all[:].bitcast(I32), 0)
-        nc.gpsimd.memset(w1s_raw[:].bitcast(I32), 0)
-        nc.gpsimd.memset(w23s_raw[:].bitcast(I32), 0)
+        def deal(engine, raw, dtype, name, run):
+            dealt = keep.tile([P, S], dtype, name=name, align_bytes=ALIGN)
+            engine.tensor_copy(
+                dealt[:].rearrange("p (t c i) -> p c t i", t=PLANES, i=run),
+                raw[:].rearrange("p (c i t) -> p c t i", t=PLANES, i=run),
+            )
+            return dealt
 
-        xw_all = keep.tile([P, T], I32, align_bytes=64)
-        w1w_raw = keep.tile([P, S], I32, align_bytes=64)
-        w23w_raw = keep.tile([P, 2, S], I32, align_bytes=64)
-        gn_sb = keep.tile([P, PACK], F32)
-        gm_sb = keep.tile([P, PACK], F32)
+        def product(out, w_words, w_scales, first, t, rhs_words, rhs_scales):
+            cols = slice(t * P, (t + 1) * P)
+            nc.tensor.matmul_mx(
+                out=out, lhsT=w_words[:, cols].bitcast(FP8X4), lhsT_scale=w_scales[first:P, cols],
+                rhs=rhs_words.bitcast(FP8X4), rhs_scale=rhs_scales, start=True, stop=True,
+            )
+
+        def quantize(words, scales, woven):
+            nc.vector.quantize_mx(out=words.bitcast(FP8X4), scales=scales, in_=woven.rearrange("p n t -> p (n t)"))
+
+        xs_all = keep.tile([P, T], U8, align_bytes=ALIGN)
+        w1s_raw = keep.tile([P, S], U8, align_bytes=ALIGN)
+        w23s_raw = keep.tile([P, S], U8, align_bytes=ALIGN)
+        nc.gpsimd.memset(xs_all[:].bitcast(I32), 0)
+        nc.vector.memset(w1s_raw[:].bitcast(I32), 0)
+        nc.vector.memset(w23s_raw[:].bitcast(I32), 0)
+
+        xw_all = keep.tile([P, T], I32, align_bytes=ALIGN)
+        w1w_raw = keep.tile([P, S], I32, align_bytes=ALIGN)
+        w23w_raw = keep.tile([P, 2, S], I32, align_bytes=ALIGN)
+        gn_sb = keep.tile([P, PLANES], F32)
+        gm_sb = keep.tile([P, PLANES], F32)
 
         load_words(w1w_raw[:], w1_words)
         l_offs = load_list(offs, "l_offs")
-        load_scales(w1s_raw, w1_scales, 0, (0,))
-        load_scales(xs_all, x_scales, 0, range(4))
+        load_scales(xs_all, x_scales, 0)
         load_words(xw_all[:], x_words)
-        load_scales(w1s_raw, w1_scales, 0, (1, 2, 3))
-        nc.gpsimd.dma_start(gn_sb[:], gn.rearrange("(p t) o -> p (t o)", t=PACK))
-        nc.gpsimd.dma_start(gm_sb[:], gm.rearrange("(p t) o -> p (t o)", t=PACK))
+        load_scales(w1s_raw, w1_scales, W1_FIRST)
+        nc.gpsimd.dma_start(gn_sb[:], gn.rearrange("(p t) o -> p (t o)", t=PLANES))
+        nc.gpsimd.dma_start(gm_sb[:], gm.rearrange("(p t) o -> p (t o)", t=PLANES))
         l1 = load_list(n1, "l1")
         l3 = load_list(n3, "l3")
         load_words(w23w_raw[:, 0, :], w2_words)
         load_words(w23w_raw[:, 1, :], w3_words)
         l2 = load_list(n2, "l2")
         l4 = load_list(n4, "l4")
-        load_scales(w23s_raw, w2_scales, 4, range(4))
-        load_scales(w23s_raw, w3_scales, 8, range(4))
+        load_scales(w23s_raw, w2_scales, W2_FIRST)
+        load_scales(w23s_raw, w3_scales, W3_FIRST)
         l5 = load_list(n5, "l5")
         l6 = load_list(n6, "l6")
         l7 = load_list(n7, "l7")
@@ -73,51 +100,47 @@ def tile_picked_forkputbdetbond_none_po_kernel(
 
         ident = keep.tile([P, P], F32)
         make_identity(nc, ident[:])
-        gain = keep.tile([P, PACK], F32)
+        gain = keep.tile([P, PLANES], F32)
         nc.scalar.activation(gain[:], gn_sb[:], COPY, scale=0.75)
 
-        def deal(raw, dtype, name, run):
-            dealt = keep.tile([P, S], dtype, name=name, align_bytes=64)
-            nc.vector.tensor_copy(dealt[:].rearrange("p (t c i) -> p c t i", t=PACK, i=run), raw[:].rearrange("p (c i t) -> p c t i", t=PACK, i=run))
-            return dealt
+        w1w = deal(nc.vector, w1w_raw, I32, "w1w", LINE_BYTES // 4)
+        w1s = deal(nc.vector, w1s_raw, U8, "w1s", LINE_BYTES)
 
-        w1w = deal(w1w_raw, I32, "w1w", 4)
-        w1s = deal(w1s_raw, U8, "w1s", 16)
-
-        xs = keep.tile([P, S], U8, align_bytes=64)
-        xw = keep.tile([P, S], U32, align_bytes=64)
+        xs = keep.tile([P, S], U8, align_bytes=ALIGN)
+        xw = keep.tile([P, S], U32, align_bytes=ALIGN)
         nc.vector.tensor_copy(xs[:], xs_all[:].indirect(l_offs[:]))
-        for h in range(2):
-            nc.vector.tensor_copy(xw[:, h * W : (h + 1) * W], xw_all[:].bitcast(U32).indirect(l_offs[:, h * 16 : (h + 1) * 16]))
-
-        def product(out, ww, ws, first, t, rw, rs):
-            cols = slice(t * P, (t + 1) * P)
-            nc.tensor.matmul_mx(out=out, lhsT=ww[:, cols].bitcast(FP8X4), lhsT_scale=ws[first:P, cols],
-                                rhs=rw.bitcast(FP8X4), rhs_scale=rs, start=True, stop=True)
+        for half in HALVES:
+            entries = l_offs[:, half.start // 16 : half.stop // 16]
+            nc.vector.tensor_copy(xw[:, half], xw_all[:].bitcast(U32).indirect(entries))
 
         y, yg = [], []
-        for t in range(PACK):
+        for t in range(PLANES):
             y.append(keep.tile([P, 2 * S], F32, name=f"y{t}"))
-            yg.append(keep.tile([P, 2 * S], F32, name=f"yg{t}", tag=f"yg{t}", align_bytes=64))
-            parts = [slice(0, W), slice(W, S)] if t == 0 else [slice(0, S)]
+            yg.append(keep.tile([P, 2 * S], F32, name=f"yg{t}", tag=f"yg{t}", align_bytes=ALIGN))
+            parts = HALVES if t == 0 else (slice(0, S),)
             banks = []
             for part in parts:
                 ps = mm.tile([P, part.stop - part.start], F32, name="ps", tag="ps")
-                product(ps[:], w1w, w1s, 0, t, xw[:, part], xs[:, part])
+                product(ps[:], w1w, w1s, W1_FIRST, t, xw[:, part], xs[:, part])
                 nc.scalar.activation(yg[t][:, part], ps[:], COPY, scale=gain[:, t : t + 1])
                 banks.append(ps)
             for part, ps in zip(parts, banks):
                 nc.scalar.copy(y[t][:, part], ps[:])
 
-        w23w = keep.tile([P, 2, S], I32, align_bytes=64)
-        nc.vector.tensor_copy(w23w[:].rearrange("p w (t c i) -> p w c t i", t=PACK, i=4), w23w_raw[:].rearrange("p w (c i t) -> p w c t i", t=PACK, i=4))
+        w23w = keep.tile([P, 2, S], I32, align_bytes=ALIGN)
+        nc.vector.tensor_copy(
+            w23w[:].rearrange("p w (t c i) -> p w c t i", t=PLANES, i=LINE_BYTES // 4),
+            w23w_raw[:].rearrange("p w (c i t) -> p w c t i", t=PLANES, i=LINE_BYTES // 4),
+        )
         w2w, w3w = w23w[:, 0, :], w23w[:, 1, :]
-        w23s = deal(w23s_raw, U8, "w23s", 16)
+        w23s = deal(nc.gpsimd, w23s_raw, U8, "w23s", LINE_BYTES)
 
         blocks = S // P
-        sums = [fwd.tile([P, PACK, P], F32, name="sums", tag="sums") for j in range(blocks)]
-        for t in range(PACK):
-            g1, g2, g3, g4, p12, p34 = [keep.tile([P, S], F32, name=f"{n}_{t}") for n in ("g1", "g2", "g3", "g4", "p12", "p34")]
+        sums = [fwd.tile([P, PLANES, P], F32, name="sums", tag="sums") for j in range(blocks)]
+        for t in range(PLANES):
+            g1, g2, g3, g4, p12, p34 = [
+                keep.tile([P, S], F32, name=f"{n}_{t}") for n in ("g1", "g2", "g3", "g4", "p12", "p34")
+            ]
             nc.vector.tensor_copy(g1[:], yg[t][:].indirect(l1[:]))
             nc.vector.tensor_scalar(g3[:], yg[t][:].indirect(l3[:]), -1.0, 0.0, MULT, ADD)
             nc.vector.tensor_copy(g2[:], y[t][:].indirect(l2[:]))
@@ -128,33 +151,35 @@ def tile_picked_forkputbdetbond_none_po_kernel(
                 blk = slice(j * P, (j + 1) * P)
                 nc.tensor.matmul(sums[j][:, t, :], p12[:, blk], ident[:], start=True, stop=False, is_transpose=True)
                 nc.tensor.matmul(sums[j][:, t, :], p34[:, blk], ident[:], start=False, stop=True, is_transpose=True)
-        z = keep.tile([P, S, PACK], BF16, name="z", tag="z", align_bytes=64)
-        z_words = z[:].rearrange("p n t -> p (n t)").bitcast(F32).rearrange("p (h j s u) -> p h j s u", h=2, u=2, s=P)
+
+        z = keep.tile([P, S, PLANES], BF16, name="z", tag="z", align_bytes=ALIGN)
+        z_pairs = z[:].rearrange("p n t -> p (n t)").bitcast(F32).rearrange("p (h j s u) -> p h j s u", h=2, u=2, s=P)
         for h in range(2):
             turned = mm.tile([P, 2, 2, P], F32, name="turned", tag="ps")
             for j in range(2):
-                zt = keep.tile([P, 2, P, 2], BF16, name=f"zt{h}{j}", tag=f"z2{j}" if h else f"zt{j}", align_bytes=64)
+                zt = keep.tile([P, 2, P, 2], BF16, name=f"zt{h}{j}", tag=f"z2{j}" if h else f"zt{j}", align_bytes=ALIGN)
                 nc.scalar.copy(zt[:], sums[2 * h + j][:].rearrange("s (u e) p -> s u p e", e=2))
-                words = zt[:].rearrange("s u p e -> s (u p e)").bitcast(F32)
+                pairs = zt[:].rearrange("s u p e -> s (u p e)").bitcast(F32)
                 for u in range(2):
-                    nc.tensor.transpose(turned[:, j, u, :], words[:, u * P : (u + 1) * P], ident[:])
-            nc.scalar.copy(z_words[:, h], turned[:].rearrange("p j u s -> p j s u"))
-        zw = keep.tile([P, S], U32, name="zw", tag="zw", align_bytes=64)
-        zs = keep.tile([P, S], U8, align_bytes=64)
-        nc.vector.quantize_mx(out=zw[:].bitcast(FP8X4), scales=zs[:], in_=z[:].rearrange("p n t -> p (n t)"))
-        a = [keep.tile([P, S], F32, name=f"a{t}") for t in range(PACK)]
-        for t in range(PACK):
+                    nc.tensor.transpose(turned[:, j, u, :], pairs[:, u * P : (u + 1) * P], ident[:])
+            nc.scalar.copy(z_pairs[:, h], turned[:].rearrange("p j u s -> p j s u"))
+        zw = keep.tile([P, S], U32, align_bytes=ALIGN)
+        zs = keep.tile([P, S], U8, align_bytes=ALIGN)
+        quantize(zw[:], zs[:], z[:])
+
+        a = [keep.tile([P, S], F32, name=f"a{t}") for t in range(PLANES)]
+        for t in range(PLANES):
             ps = mm.tile([P, S], F32, name="ps", tag="ps")
-            product(ps[:], w2w, w23s, 4, t, zw[:], zs[:])
+            product(ps[:], w2w, w23s, W2_FIRST, t, zw[:], zs[:])
             nc.scalar.copy(a[t][:], ps[:])
 
-        z2 = [keep.tile([P, W, PACK], BF16, name=f"z2{h}", tag=f"z2{h}", align_bytes=64) for h in range(2)]
-        early = keep.tile([P, 5, W], F32, name="early", tag="yg3", align_bytes=64)
-        late = keep.tile([P, 2, W], F32, name="late", tag="z", align_bytes=64)
-        pa2 = keep.tile([P, W], F32, name="pa2", tag="pa2", align_bytes=64)
+        z2 = [keep.tile([P, W, PLANES], BF16, name=f"z2{h}", tag=f"z2{h}", align_bytes=ALIGN) for h in range(2)]
+        early = keep.tile([P, 5, W], F32, name="early", tag="yg3", align_bytes=ALIGN)
+        late = keep.tile([P, 2, W], F32, name="late", tag="z", align_bytes=ALIGN)
+        pa2 = keep.tile([P, W], F32, name="pa2", tag="pa2", align_bytes=ALIGN)
         pa = [early[:, 0, :], early[:, 2, :], pa2[:], early[:, 4, :]]
         pb = [early[:, 1, :], early[:, 3, :], late[:, 0, :], late[:, 1, :]]
-        dt = [keep.tile([P, S], F32, name=f"dt{t}", tag=f"dt{t}", align_bytes=64) for t in range(PACK)]
+        dt = [keep.tile([P, S], F32, name=f"dt{t}", tag=f"dt{t}", align_bytes=ALIGN) for t in range(PLANES)]
 
         def fetch_a(t):
             nc.vector.tensor_copy(pa[t], y[t][:].indirect(l5[:]))
@@ -167,8 +192,8 @@ def tile_picked_forkputbdetbond_none_po_kernel(
 
         def put_product(t):
             nc.vector.tensor_tensor(dt[t][:].indirect(l6[:]), pa[t], pb[t], MULT)
-            for h in range(2):
-                nc.scalar.activation(z2[h][:, :, t], dt[t][:, h * W : (h + 1) * W], COPY, scale=gm_sb[:, t : t + 1])
+            for h, half in enumerate(HALVES):
+                nc.scalar.activation(z2[h][:, :, t], dt[t][:, half], COPY, scale=gm_sb[:, t : t + 1])
 
         fetch_a(0)
         fetch_b(0)
@@ -187,11 +212,11 @@ def tile_picked_forkputbdetbond_none_po_kernel(
         put_product(2)
         put_product(3)
 
-        z2w = keep.tile([P, S], U32, align_bytes=64)
-        z2s = keep.tile([P, S], U8, align_bytes=64)
-        b = [keep.tile([P, S], F32, name=f"b{t}") for t in range(PACK)]
-        own01 = keep.tile([P, 2, W], F32, name="own01", tag="pa2", align_bytes=64)
-        own23 = keep.tile([P, 2, W], F32, name="own23", tag="dt3", align_bytes=64)
+        z2w = keep.tile([P, S], U32, align_bytes=ALIGN)
+        z2s = keep.tile([P, S], U8, align_bytes=ALIGN)
+        b = [keep.tile([P, S], F32, name=f"b{t}") for t in range(PLANES)]
+        own01 = keep.tile([P, 2, W], F32, name="own01", tag="pa2", align_bytes=ALIGN)
+        own23 = keep.tile([P, 2, W], F32, name="own23", tag="dt3", align_bytes=ALIGN)
         ga = [own01[:, 0, :], own01[:, 1, :], own23[:, 0, :], own23[:, 1, :]]
 
         def fetch_own(t):
@@ -199,41 +224,40 @@ def tile_picked_forkputbdetbond_none_po_kernel(
 
         fetch_own(0)
         fetch_own(1)
-        for h in range(2):
-            half = slice(h * W, (h + 1) * W)
-            nc.vector.quantize_mx(out=z2w[:, half].bitcast(FP8X4), scales=z2s[:, half], in_=z2[h][:].rearrange("p n t -> p (n t)"))
+        for h, half in enumerate(HALVES):
+            quantize(z2w[:, half], z2s[:, half], z2[h][:])
             for t in range(2):
                 ps = mm.tile([P, W], F32, name="ps", tag="ps")
-                product(ps[:], w3w, w23s, 8, t, z2w[:, half], z2s[:, half])
+                product(ps[:], w3w, w23s, W3_FIRST, t, z2w[:, half], z2s[:, half])
                 nc.scalar.copy(b[t][:, half], ps[:])
         fetch_own(2)
         fetch_own(3)
-        for t in range(2, PACK):
+        for t in range(2, PLANES):
             ps = fwd.tile([P, S], F32, name="whole", tag="sums")
-            product(ps[:], w3w, w23s, 8, t, z2w[:], z2s[:])
+            product(ps[:], w3w, w23s, W3_FIRST, t, z2w[:], z2s[:])
             nc.scalar.copy(b[t][:], ps[:])
 
-        res = [keep.tile([P, W, PACK], BF16, name=f"res{h}", align_bytes=64) for h in range(2)]
-        rows = out_0.rearrange("(p t) n -> p t n", t=PACK)
-        gb = [keep.tile([P, W], F32, name=f"gb{t}") for t in range(PACK)]
+        res = [keep.tile([P, W, PLANES], BF16, name=f"res{h}", align_bytes=ALIGN) for h in range(2)]
+        rows = out_0.rearrange("(p t) n -> p t n", t=PLANES)
+        gb = [keep.tile([P, W], F32, name=f"gb{t}") for t in range(PLANES)]
         nc.vector.tensor_copy(gb[0][:], b[0][:].indirect(l8[:]))
-        for t in range(PACK):
-            if t + 1 < PACK:
+        for t in range(PLANES):
+            if t + 1 < PLANES:
                 nc.vector.tensor_copy(gb[t + 1][:], b[t + 1][:].indirect(l8[:]))
             nc.vector.tensor_tensor(a[t][:].indirect(l7[:]), gb[t][:], ga[t], ADD)
             nc.sync.dma_start(rows[:, t, :], a[t][:])
             if t < 2:
-                nc.scalar.copy(res[1][:, :, t], a[t][:, W:S])
-            nc.scalar.copy(res[0][:, :, t], a[t][:, 0:W])
-        for t in range(2, PACK):
-            nc.vector.tensor_copy(res[1][:, :, t], a[t][:, W:S])
-        rw = keep.tile([P, S], U32, align_bytes=64)
-        rs = keep.tile([P, S], U8, align_bytes=64)
+                nc.scalar.copy(res[1][:, :, t], a[t][:, HALVES[1]])
+            nc.scalar.copy(res[0][:, :, t], a[t][:, HALVES[0]])
+        for t in range(2, PLANES):
+            nc.vector.tensor_copy(res[1][:, :, t], a[t][:, HALVES[1]])
+
+        res_words = keep.tile([P, S], U32, align_bytes=ALIGN)
+        res_scales = keep.tile([P, S], U8, align_bytes=ALIGN)
         words_out = out_1[0].rearrange("p n r -> p (n r)").bitcast(I32)
-        for h in range(2):
-            half = slice(h * W, (h + 1) * W)
-            nc.vector.quantize_mx(out=rw[:, half].bitcast(FP8X4), scales=rs[:, half], in_=res[h][:].rearrange("p n t -> p (n t)"))
-            nc.sync.dma_start(words_out[:, half], rw[:, half].bitcast(I32))
-        for q in range(4):
+        for h, half in enumerate(HALVES):
+            quantize(res_words[:, half], res_scales[:, half], res[h][:])
+            nc.sync.dma_start(words_out[:, half], res_words[:, half].bitcast(I32))
+        for q in range(QUADRANTS):
             queue = nc.scalar if q % 2 else nc.sync
-            queue.dma_start(out_2[0, 4 * q : 4 * q + 4, :].bitcast(I32), rs[32 * q : 32 * q + 4, :].bitcast(I32))
+            queue.dma_start(out_2[0, 4 * q : 4 * q + 4, :].bitcast(I32), res_scales[32 * q : 32 * q + 4, :].bitcast(I32))

from contextlib import ExitStack

import concourse.mybir as mybir
from concourse.masks import make_identity

F32, BF16 = mybir.dt.float32, mybir.dt.bfloat16
I32, U32, U16, U8 = mybir.dt.int32, mybir.dt.uint32, mybir.dt.uint16, mybir.dt.uint8
FP8X4 = mybir.dt.float8_e4m3fn_x4
MULT, ADD = mybir.AluOpType.mult, mybir.AluOpType.add
COPY = mybir.ActivationFunctionType.Copy

P = 128
PLANES = 4
QUADRANTS = 4
T = 2048
S = 512
W = 256
HALVES = (slice(0, W), slice(W, S))
W1_FIRST, W2_FIRST, W3_FIRST = 0, 4, 8
LINE_BYTES = 16
BANKS = 4
ALIGN = 64
FLOPS = 3 * 2 * 512 * 512 * 512


def tile_picked_forkputbdetbond_none_po_kernel(
    tc, x_words, x_scales, w1_words, w1_scales, gn, w2_words, w2_scales, gm, w3_words, w3_scales,
    offs, n1, n2, n3, n4, n5, n6, n7, n8, out_0, out_1, out_2,
):
    nc = tc.nc
    with ExitStack() as ctx:
        keep = ctx.enter_context(tc.tile_pool(name="keep", bufs=1))
        mm = ctx.enter_context(tc.psum_pool(name="mm", bufs=BANKS))
        fwd = ctx.enter_context(tc.psum_pool(name="fwd", bufs=BANKS))

        def load_list(src, name):
            tile = keep.tile([P, src.shape[1]], U16, name=name)
            nc.sync.dma_start(tile[:], src)
            return tile

        def load_words(dst, src):
            nc.sync.dma_start(dst, src[0].rearrange("p n r -> p (n r)").bitcast(I32))

        def load_scales(dst, src, first):
            for q in range(QUADRANTS):
                nc.sync.dma_start(
                    dst[32 * q + first : 32 * q + first + 4, :].bitcast(I32), src[0, 4 * q : 4 * q + 4, :].bitcast(I32)
                )

        def deal(engine, raw, dtype, name, run):
            dealt = keep.tile([P, S], dtype, name=name, align_bytes=ALIGN)
            engine.tensor_copy(
                dealt[:].rearrange("p (t c i) -> p c t i", t=PLANES, i=run),
                raw[:].rearrange("p (c i t) -> p c t i", t=PLANES, i=run),
            )
            return dealt

        def product(out, w_words, w_scales, first, t, rhs_words, rhs_scales):
            cols = slice(t * P, (t + 1) * P)
            nc.tensor.matmul_mx(
                out=out, lhsT=w_words[:, cols].bitcast(FP8X4), lhsT_scale=w_scales[first:P, cols],
                rhs=rhs_words.bitcast(FP8X4), rhs_scale=rhs_scales, start=True, stop=True,
            )

        def quantize(words, scales, woven):
            nc.vector.quantize_mx(out=words.bitcast(FP8X4), scales=scales, in_=woven.rearrange("p n t -> p (n t)"))

        xs_all = keep.tile([P, T], U8, align_bytes=ALIGN)
        w1s_raw = keep.tile([P, S], U8, align_bytes=ALIGN)
        w23s_raw = keep.tile([P, S], U8, align_bytes=ALIGN)
        nc.gpsimd.memset(xs_all[:].bitcast(I32), 0)
        nc.vector.memset(w1s_raw[:].bitcast(I32), 0)
        nc.vector.memset(w23s_raw[:].bitcast(I32), 0)

        xw_all = keep.tile([P, T], I32, align_bytes=ALIGN)
        w1w_raw = keep.tile([P, S], I32, align_bytes=ALIGN)
        w23w_raw = keep.tile([P, 2, S], I32, align_bytes=ALIGN)
        gn_sb = keep.tile([P, PLANES], F32)
        gm_sb = keep.tile([P, PLANES], F32)

        load_words(w1w_raw[:], w1_words)
        l_offs = load_list(offs, "l_offs")
        load_scales(xs_all, x_scales, 0)
        load_words(xw_all[:], x_words)
        load_scales(w1s_raw, w1_scales, W1_FIRST)
        nc.gpsimd.dma_start(gn_sb[:], gn.rearrange("(p t) o -> p (t o)", t=PLANES))
        nc.gpsimd.dma_start(gm_sb[:], gm.rearrange("(p t) o -> p (t o)", t=PLANES))
        l1 = load_list(n1, "l1")
        l3 = load_list(n3, "l3")
        load_words(w23w_raw[:, 0, :], w2_words)
        load_words(w23w_raw[:, 1, :], w3_words)
        l2 = load_list(n2, "l2")
        l4 = load_list(n4, "l4")
        load_scales(w23s_raw, w2_scales, W2_FIRST)
        load_scales(w23s_raw, w3_scales, W3_FIRST)
        l5 = load_list(n5, "l5")
        l6 = load_list(n6, "l6")
        l7 = load_list(n7, "l7")
        l8 = load_list(n8, "l8")

        ident = keep.tile([P, P], F32)
        make_identity(nc, ident[:])
        gain = keep.tile([P, PLANES], F32)
        nc.scalar.activation(gain[:], gn_sb[:], COPY, scale=0.75)

        w1w = deal(nc.vector, w1w_raw, I32, "w1w", LINE_BYTES // 4)
        w1s = deal(nc.vector, w1s_raw, U8, "w1s", LINE_BYTES)

        xs = keep.tile([P, S], U8, align_bytes=ALIGN)
        xw = keep.tile([P, S], U32, align_bytes=ALIGN)
        nc.vector.tensor_copy(xs[:], xs_all[:].indirect(l_offs[:]))
        for half in HALVES:
            entries = l_offs[:, half.start // 16 : half.stop // 16]
            nc.vector.tensor_copy(xw[:, half], xw_all[:].bitcast(U32).indirect(entries))

        y, yg = [], []
        for t in range(PLANES):
            y.append(keep.tile([P, 2 * S], F32, name=f"y{t}"))
            yg.append(keep.tile([P, 2 * S], F32, name=f"yg{t}", tag=f"yg{t}", align_bytes=ALIGN))
            parts = HALVES if t == 0 else (slice(0, S),)
            banks = []
            for part in parts:
                ps = mm.tile([P, part.stop - part.start], F32, name="ps", tag="ps")
                product(ps[:], w1w, w1s, W1_FIRST, t, xw[:, part], xs[:, part])
                nc.scalar.activation(yg[t][:, part], ps[:], COPY, scale=gain[:, t : t + 1])
                banks.append(ps)
            for part, ps in zip(parts, banks):
                nc.scalar.copy(y[t][:, part], ps[:])

        w23w = keep.tile([P, 2, S], I32, align_bytes=ALIGN)
        nc.vector.tensor_copy(
            w23w[:].rearrange("p w (t c i) -> p w c t i", t=PLANES, i=LINE_BYTES // 4),
            w23w_raw[:].rearrange("p w (c i t) -> p w c t i", t=PLANES, i=LINE_BYTES // 4),
        )
        w2w, w3w = w23w[:, 0, :], w23w[:, 1, :]
        w23s = deal(nc.gpsimd, w23s_raw, U8, "w23s", LINE_BYTES)

        blocks = S // P
        sums = [fwd.tile([P, PLANES, P], F32, name="sums", tag="sums") for j in range(blocks)]
        for t in range(PLANES):
            g1, g2, g3, g4, p12, p34 = [
                keep.tile([P, S], F32, name=f"{n}_{t}") for n in ("g1", "g2", "g3", "g4", "p12", "p34")
            ]
            nc.vector.tensor_copy(g1[:], yg[t][:].indirect(l1[:]))
            nc.vector.tensor_scalar(g3[:], yg[t][:].indirect(l3[:]), -1.0, 0.0, MULT, ADD)
            nc.vector.tensor_copy(g2[:], y[t][:].indirect(l2[:]))
            nc.vector.tensor_copy(g4[:], y[t][:].indirect(l4[:]))
            nc.gpsimd.tensor_tensor(p12[:], g1[:], g2[:], MULT)
            nc.gpsimd.tensor_tensor(p34[:], g3[:], g4[:], MULT)
            for j in range(blocks):
                blk = slice(j * P, (j + 1) * P)
                nc.tensor.matmul(sums[j][:, t, :], p12[:, blk], ident[:], start=True, stop=False, is_transpose=True)
                nc.tensor.matmul(sums[j][:, t, :], p34[:, blk], ident[:], start=False, stop=True, is_transpose=True)

        z = keep.tile([P, S, PLANES], BF16, name="z", tag="z", align_bytes=ALIGN)
        z_pairs = z[:].rearrange("p n t -> p (n t)").bitcast(F32).rearrange("p (h j s u) -> p h j s u", h=2, u=2, s=P)
        for h in range(2):
            turned = mm.tile([P, 2, 2, P], F32, name="turned", tag="ps")
            for j in range(2):
                zt = keep.tile([P, 2, P, 2], BF16, name=f"zt{h}{j}", tag=f"z2{j}" if h else f"zt{j}", align_bytes=ALIGN)
                nc.scalar.copy(zt[:], sums[2 * h + j][:].rearrange("s (u e) p -> s u p e", e=2))
                pairs = zt[:].rearrange("s u p e -> s (u p e)").bitcast(F32)
                for u in range(2):
                    nc.tensor.transpose(turned[:, j, u, :], pairs[:, u * P : (u + 1) * P], ident[:])
            nc.scalar.copy(z_pairs[:, h], turned[:].rearrange("p j u s -> p j s u"))
        zw = keep.tile([P, S], U32, align_bytes=ALIGN)
        zs = keep.tile([P, S], U8, align_bytes=ALIGN)
        quantize(zw[:], zs[:], z[:])

        a = [keep.tile([P, S], F32, name=f"a{t}") for t in range(PLANES)]
        for t in range(PLANES):
            ps = mm.tile([P, S], F32, name="ps", tag="ps")
            product(ps[:], w2w, w23s, W2_FIRST, t, zw[:], zs[:])
            nc.scalar.copy(a[t][:], ps[:])

        z2 = [keep.tile([P, W, PLANES], BF16, name=f"z2{h}", tag=f"z2{h}", align_bytes=ALIGN) for h in range(2)]
        early = keep.tile([P, 5, W], F32, name="early", tag="yg3", align_bytes=ALIGN)
        late = keep.tile([P, 2, W], F32, name="late", tag="z", align_bytes=ALIGN)
        pa2 = keep.tile([P, W], F32, name="pa2", tag="pa2", align_bytes=ALIGN)
        pa = [early[:, 0, :], early[:, 2, :], pa2[:], early[:, 4, :]]
        pb = [early[:, 1, :], early[:, 3, :], late[:, 0, :], late[:, 1, :]]
        dt = [keep.tile([P, S], F32, name=f"dt{t}", tag=f"dt{t}", align_bytes=ALIGN) for t in range(PLANES)]

        def fetch_a(t):
            nc.vector.tensor_copy(pa[t], y[t][:].indirect(l5[:]))

        def fetch_b(t):
            nc.vector.tensor_copy(pb[t], y[t][:].indirect(l6[:]))

        def put_sum(t):
            nc.vector.tensor_tensor(dt[t][:].indirect(l5[:]), pa[t], pb[t], ADD)

        def put_product(t):
            nc.vector.tensor_tensor(dt[t][:].indirect(l6[:]), pa[t], pb[t], MULT)
            for h, half in enumerate(HALVES):
                nc.scalar.activation(z2[h][:, :, t], dt[t][:, half], COPY, scale=gm_sb[:, t : t + 1])

        fetch_a(0)
        fetch_b(0)
        fetch_a(1)
        put_sum(0)
        fetch_b(1)
        put_product(0)
        fetch_a(2)
        put_sum(1)
        fetch_a(3)
        put_product(1)
        fetch_b(2)
        fetch_b(3)
        put_sum(2)
        put_sum(3)
        put_product(2)
        put_product(3)

        z2w = keep.tile([P, S], U32, align_bytes=ALIGN)
        z2s = keep.tile([P, S], U8, align_bytes=ALIGN)
        b = [keep.tile([P, S], F32, name=f"b{t}") for t in range(PLANES)]
        own01 = keep.tile([P, 2, W], F32, name="own01", tag="pa2", align_bytes=ALIGN)
        own23 = keep.tile([P, 2, W], F32, name="own23", tag="dt3", align_bytes=ALIGN)
        ga = [own01[:, 0, :], own01[:, 1, :], own23[:, 0, :], own23[:, 1, :]]

        def fetch_own(t):
            nc.vector.tensor_scalar(ga[t], a[t][:].indirect(l7[:]), -0.5, 0.0, MULT, ADD)

        fetch_own(0)
        fetch_own(1)
        for h, half in enumerate(HALVES):
            quantize(z2w[:, half], z2s[:, half], z2[h][:])
            for t in range(2):
                ps = mm.tile([P, W], F32, name="ps", tag="ps")
                product(ps[:], w3w, w23s, W3_FIRST, t, z2w[:, half], z2s[:, half])
                nc.scalar.copy(b[t][:, half], ps[:])
        fetch_own(2)
        fetch_own(3)
        for t in range(2, PLANES):
            ps = fwd.tile([P, S], F32, name="whole", tag="sums")
            product(ps[:], w3w, w23s, W3_FIRST, t, z2w[:], z2s[:])
            nc.scalar.copy(b[t][:], ps[:])

        res = [keep.tile([P, W, PLANES], BF16, name=f"res{h}", align_bytes=ALIGN) for h in range(2)]
        rows = out_0.rearrange("(p t) n -> p t n", t=PLANES)
        gb = [keep.tile([P, W], F32, name=f"gb{t}") for t in range(PLANES)]
        nc.vector.tensor_copy(gb[0][:], b[0][:].indirect(l8[:]))
        for t in range(PLANES):
            if t + 1 < PLANES:
                nc.vector.tensor_copy(gb[t + 1][:], b[t + 1][:].indirect(l8[:]))
            nc.vector.tensor_tensor(a[t][:].indirect(l7[:]), gb[t][:], ga[t], ADD)
            nc.sync.dma_start(rows[:, t, :], a[t][:])
            if t < 2:
                nc.scalar.copy(res[1][:, :, t], a[t][:, HALVES[1]])
            nc.scalar.copy(res[0][:, :, t], a[t][:, HALVES[0]])
        for t in range(2, PLANES):
            nc.vector.tensor_copy(res[1][:, :, t], a[t][:, HALVES[1]])

        res_words = keep.tile([P, S], U32, align_bytes=ALIGN)
        res_scales = keep.tile([P, S], U8, align_bytes=ALIGN)
        words_out = out_1[0].rearrange("p n r -> p (n r)").bitcast(I32)
        for h, half in enumerate(HALVES):
            quantize(res_words[:, half], res_scales[:, half], res[h][:])
            nc.sync.dma_start(words_out[:, half], res_words[:, half].bitcast(I32))
        for q in range(QUADRANTS):
            queue = nc.scalar if q % 2 else nc.sync
            queue.dma_start(out_2[0, 4 * q : 4 * q + 4, :].bitcast(I32), res_scales[32 * q : 32 * q + 4, :].bitcast(I32))
